import numpy as np
CORES = [16,17,18,19,150,151]
N = 6
W, TIMES = 512, 3
def setup_inputs(rng):
    return {"b": rng.standard_normal((N, 128, W), dtype=np.float32)}
def op(p):
    return 3.0 * p - (np.roll(p, 1, 1) + np.roll(p, -1, 1)) - 0.25 * (np.roll(p, 2, 1) + np.roll(p, -2, 1))
def reference(b):
    e = np.concatenate(list(b.astype(np.float64)), axis=1)
    x = np.zeros_like(e); p = e.copy(); ee = (e * e).sum(axis=1, keepdims=True)
    for _ in range(TIMES):
        q = op(p)
        al = ee / (p * q).sum(axis=1, keepdims=True)
        x = x + al * p; e = e - al * q
        en = (e * e).sum(axis=1, keepdims=True)
        p = e + (en / ee) * p; ee = en
    return {"y": np.stack([x[:, W * i:W * i + W] for i in range(N)]).astype(np.float32)}

@@ -1,0 +1,298 @@
+import math
+from concourse.bass import DstId, RemoteDMATransfer
+from concourse.mybir import AluOpType, AxisListType, ActivationFunctionType
+
+W, HALO = 512, 10
+WX = W + HALO
+XS = [0, 192, 384, 448, WX]
+LD = 384
+YS = [0, 320, W]
+LEV = ["B", "H1", "W1", "XX", "W2", "H3"]
+R18 = math.sqrt(18.0)
+ALPHA = [None, 2.0, 2.0, R18 + 2.0, R18 - 2.0, 2.0]
+SQ = 2.0 ** -8
+SLOT = 16
+DQ = {}
+TINY, EARLY = "s", 4
+
+SCRATCH = {"ACC": ("sbuf", [128, 48], "float32"), "R": ("sbuf", [128, 6 * SLOT], "float32"),
+           "T1": ("sbuf", [128, 3 * SLOT], "float32"), "T2": ("sbuf", [128, SLOT], "float32"),
+           "Z": ("sbuf", [128, SLOT], "float32"), "SM": ("sbuf", [128, 64], "float32"),
+           "JT": ("sbuf", [128, 48], "float32"),
+           "Y": ("sbuf", [128, W], "float32"), "PR": ("sbuf", [128, WX], "float32")}
+for _n in LEV + ["J0", "J1", "J2", "J3", "J4", "J5"]:
+    SCRATCH[_n] = ("sbuf", [128, WX], "float32")
+for _j in range(4):
+    SCRATCH["pd%d" % _j] = ("psum", [128, 512], "float32")
+    SCRATCH["pf%d" % _j] = ("psum", [128, 512], "float32")
+SEMAPHORES = ["ld1", "ld2", "halo", "arr", "sent", "st1", "st2", "vdone", "sdone"]
+
+
+def _bits(m):
+    return sum((m >> i) & 1 for i in range(32))
+
+
+def rank_program(g, core, T, topo):
+    rank = T.rank_of(core)
+    if rank is None:
+        return
+    cores = list(T.cores)
+    n = len(cores)
+    left, right = cores[(rank - 1) % n], cores[(rank + 1) % n]
+    A, F = AluOpType, ActivationFunctionType
+    queues = {"v": g.vector, "s": g.scalar, "g": g, "y": g.sync}
+    hist, count = [], {}
+    seen = {"v": {}, "s": {}, "g": {}, "y": {}}
+
+    def ap(r):
+        return T[r[0]][:, r[1]:r[2]]
+
+    def over(a, b, bank):
+        if a[0] != b[0]:
+            return False
+        return (bank and a[0][0] == "p") or (a[1] < b[2] and b[1] < a[2])
+
+    def clash(q, reads, writes, h):
+        other = q != h[0]
+        for x in writes:
+            for o in h[3] + h[4]:
+                if over(x, o, other):
+                    return True
+        for x in reads:
+            for o in h[4]:
+                if over(x, o, other):
+                    return True
+            if other and x[0][0] == "p":
+                for o in h[3]:
+                    if x[0] == o[0]:
+                        return True
+        return False
+
+    def sync_to(q, reads, writes):
+        need = {}
+        for h in hist:
+            if seen[q].get(h[1], 0) < h[2] and need.get(h[1], 0) < h[2] and clash(q, reads, writes, h):
+                need[h[1]] = h[2]
+        for s in need:
+            queues[q].wait_ge(T.sem[s], need[s])
+            seen[q][s] = need[s]
+
+    def note(q, sem, inc, reads, writes):
+        count[sem] = count.get(sem, 0) + inc
+        hist.append((q, sem, count[sem], reads, writes))
+
+    def op(q, reads, writes, fn):
+        sync_to(q, reads, writes)
+        sem = "vdone" if q == "v" else "sdone"
+        fn().then_inc(T.sem[sem], 1)
+        note(q, sem, 1, reads, writes)
+
+    def val(x):
+        return ap(x) if isinstance(x, tuple) else x
+
+    def cols(*xs):
+        return [x for x in xs if isinstance(x, tuple)]
+
+    def act(out, in_, func, scale=1.0, bias=0.0, acc=None):
+        def fn():
+            if acc is not None:
+                return g.scalar.activation(ap(out), ap(in_), func, bias=val(bias), scale=val(scale), accum_out=ap(acc))
+            return g.scalar.activation(ap(out), ap(in_), func, bias=val(bias), scale=val(scale))
+        op("s", [in_] + cols(scale, bias), [out] + cols(acc), fn)
+
+    def tt(out, a, b, o):
+        op("v", [a, b], [out], lambda: g.vector.tensor_tensor(ap(out), ap(a), ap(b), o))
+
+    def ts(out, a, s1, o1, s2=None, o2=None):
+        if o2 is None:
+            op("v", [a] + cols(s1), [out], lambda: g.vector.tensor_scalar(ap(out), ap(a), val(s1), None, o1))
+        else:
+            op("v", [a] + cols(s1, s2), [out], lambda: g.vector.tensor_scalar(ap(out), ap(a), val(s1), val(s2), o1, o2))
+
+    def red(out, a, neg=False):
+        op("v", [a], [out], lambda: g.vector.tensor_reduce(ap(out), ap(a), AxisListType.X, A.add, negate=neg))
+
+    def cpy(out, a):
+        op("v", [a], [out], lambda: g.vector.tensor_copy(ap(out), ap(a)))
+
+    def dma(sem, out, in_, reads, writes):
+        sync_to("y", reads, writes)
+        g.sync.dma_start(out, in_).then_inc(T.sem[sem], 16)
+        note("y", sem, 16, reads, writes)
+
+    own = rank * SLOT
+
+    def P(c, w=1):
+        return ("R", own + c, own + c + w)
+
+    others = [c for c in cores if c != core]
+    off = [c for c in others if (topo.host(c), topo.chip(c)) != (topo.host(core), topo.chip(core))]
+    on = [c for c in others if c not in off]
+
+    def masks(src):
+        o = [c for c in cores if c != src and (topo.host(c), topo.chip(c)) != (topo.host(src), topo.chip(src))]
+        i = [c for c in cores if c != src and c not in o]
+        mo = topo.mask(src, o[0])
+        return mo, topo.mask(src, i[0]) & ~mo
+
+    note("x", "halo", _bits(topo.mask(right, core)), [], [("B", W, WX)])
+    arrive = 0
+    for c in others:
+        mo, mi = masks(c)
+        arrive += _bits(mo if c in off else mi)
+    note("x", "arr", arrive, [], [("R", T.rank_of(c) * SLOT, T.rank_of(c) * SLOT + SLOT) for c in others])
+
+    dma("ld1", T.B[:, 0:LD], T.b[:, 0:LD], [], [("B", 0, LD)])
+    dma("ld2", T.B[:, LD:W], T.b[:, LD:W], [], [("B", LD, W)])
+    op("v", [], [P(0, SLOT)], lambda: g.vector.memset(ap(P(0, SLOT)), 0.0))
+    sync_to("g", [("B", 0, HALO)], [])
+    rid, pid = topo.addr(left, core)
+    m1 = topo.mask(core, left)
+    g.remote_dma(T.B[:, W:WX], T.B[:, 0:HALO], T.sem.halo, T.sem.sent, pid, rid, m1)
+    count["sent"] = _bits(m1)
+
+    NB = len(XS) - 1
+    last = NB - 1
+
+    def rng(j, k):
+        return (k if j == 0 else XS[j] - k), XS[j + 1] - k
+
+    def pd(j, lo, hi):
+        base = max(0, XS[j] - 8)
+        return ("pd%d" % j, lo - base, hi - base)
+
+    def scale_(j, k):
+        lo, hi = rng(j, k)
+        if DQ.get((j, k), "s" if j < 2 else "v") == "s":
+            act(pd(j, lo, hi), (LEV[k - 1], lo, hi), F.Copy, scale=ALPHA[k])
+        else:
+            ts(pd(j, lo, hi), (LEV[k - 1], lo, hi), ALPHA[k], A.mult)
+
+    def adds(j, k):
+        lo, hi = rng(j, k)
+        d, o = pd(j, lo, hi), (A.subtract if k == 4 else A.add)
+        if k == 5:
+            tt(("PR", lo, hi), ("W1", lo, hi), d, A.mult)
+        tt(d, d, (LEV[k - 1], lo - 1, hi - 1), o)
+        tt((LEV[k], lo, hi), d, (LEV[k - 1], lo + 1, hi + 1), o)
+
+    def acc(m, j):
+        return ("ACC", 8 * m + j, 8 * m + j + 1)
+
+    def sq(j, k):
+        lo, hi = rng(j, k) if k else (XS[j], XS[j + 1])
+        hi = min(hi, W + k)
+        act(("J%d" % k, lo, hi), (LEV[k], lo, hi), F.Square, scale=SQ, acc=acc(k, j))
+
+    def sp(j):
+        lo, hi = rng(j, 5)
+        act(("J3", lo, hi), ("PR", lo, hi), F.Copy, scale=0.5 * SQ * SQ, acc=acc(3, j))
+
+    def total(q, out, m, more=0, neg=False):
+        src = ("ACC", 8 * m, 8 * m + NB + more)
+        if q == "v":
+            red(out, src, neg)
+        else:
+            act(("JT", 8 * m, 8 * m + NB + more), src, F.Copy, scale=(-1.0 if neg else 1.0), acc=out)
+
+    def times(q, out, a, c):
+        if q == "v":
+            ts(out, a, c, A.mult)
+        else:
+            act(out, a, F.Copy, scale=c)
+
+    extra = {1: 1, 2: 2, 3: 0, 4: 4}
+    scale_(0, 1); scale_(1, 1)
+    adds(0, 1); adds(1, 1)
+    for k in range(1, 5):
+        scale_(0, k + 1); sq(0, extra[k]); scale_(1, k + 1); sq(1, extra[k])
+        adds(0, k + 1); adds(1, k + 1)
+    sp(0); sq(0, 5); sp(1); sq(1, 5)
+    e = TINY
+    for j in range(2, NB):
+        sq(j, 0)
+        for k in range(1, 6):
+            scale_(j, k); adds(j, k)
+            if k == 5:
+                sp(j)
+            if k != 3:
+                sq(j, k)
+            if j == last and k == 2:
+                cpy(P(10, 2), ("W1", W, W + 2))
+            if j == last and k == EARLY:
+                total(e, P(5), 0); times(e, acc(1, NB), P(5), -18.0)
+                total(e, P(1), 1); times(e, acc(2, NB), P(1), -18.0)
+                total(e, P(8), 1, 1, True); total(e, P(4), 2, 1, True); times(e, acc(3, NB), P(4), -18.0)
+            if j == last and k == 4:
+                cpy(P(12, 4), ("W2", W, W + 4))
+    total("v", P(3), 4); times("v", acc(5, NB), P(3), -18.0)
+    total("v", P(0), 3); total("v", P(6), 3, 1, True)
+    total("v", P(2), 5, 1, True)
+
+    sync_to("g", [P(0, SLOT)], [])
+    mo, mi = masks(core)
+
+    def transfer(dsts, m):
+        ids = []
+        for c in dsts:
+            r_, p_ = topo.addr(c, core)
+            ids.append(DstId(rid=r_, pnc=p_))
+        return RemoteDMATransfer(dst_ids=ids, dma_engine_mask=m, remote_sem=T.sem.arr, srcs=[ap(P(0, SLOT))],
+                                 dsts=[ap(P(0, SLOT)) for c in dsts], alu_op=0)
+
+    if mi & ~m1:
+        g.remote_dma_fused([transfer(off, mo)], local_sem=T.sem.sent)
+        g.remote_dma_fused([transfer(on, mi)], local_sem=T.sem.sent)
+    else:
+        g.remote_dma_fused([transfer(off, mo), transfer(on, mi)], local_sem=T.sem.sent)
+    count["sent"] += _bits(mo) + _bits(mi)
+
+    def S(c, w=1):
+        return ("SM", c, c + w)
+
+    def Z(c, w=1):
+        return ("Z", c, c + w)
+
+    lo_ = T.rank_of(left) * SLOT
+    act(("W1", 0, 2), ("R", lo_ + 10, lo_ + 12), F.Copy)
+    act(("W2", 0, 4), ("R", lo_ + 12, lo_ + 16), F.Copy)
+    tt(("T1", 0, 48), ("R", 0, 48), ("R", 48, 96), A.add)
+    tt(("T2", 0, 16), ("T1", 0, 16), ("T1", 16, 32), A.add)
+    tt(Z(0, 16), ("T2", 0, 16), ("T1", 32, 48), A.add)
+    act(S(8, 2), Z(4, 2), F.Copy, scale=Z(4))
+    ts(S(0, 5), Z(0, 5), Z(8), A.mult)
+    act(S(11, 2), Z(4, 2), F.Copy, scale=Z(6))
+    ts(S(10), Z(6), Z(6), A.mult)
+    act(S(32), Z(8), F.Copy)
+    act(S(42), Z(5), F.Copy, scale=-1.0)
+    tt(S(16, 5), S(0, 5), S(8, 5), A.subtract)
+    act(S(26, 2), S(19, 2), F.Copy, scale=S(19))
+    ts(S(24, 2), S(16, 2), S(18), A.mult)
+    tt(S(33, 2), S(24, 2), S(26, 2), A.subtract)
+    act(S(40), S(19), F.Copy, scale=-1.0)
+    act(S(41), S(17), F.Copy, scale=S(40))
+    act(S(35), S(16), F.Identity, scale=S(20), bias=S(41))
+    op("v", [S(32, 2)], [S(36, 2)], lambda: g.vector.reciprocal(ap(S(36, 2)), ap(S(32, 2))))
+    ts(S(45, 2), S(34, 2), S(37), A.mult, 4.0, A.mult)
+    act(S(43), S(33), F.Copy, scale=S(42))
+    act(S(48), S(34), F.Identity, scale=Z(4), bias=S(43))
+    act(S(49), S(35), F.Identity, scale=Z(6), bias=S(48))
+    ts(S(50), S(36), S(37), A.mult, -4.0, A.mult)
+    ts(S(44), S(49), S(50), A.mult)
+
+    a0, a1, a2 = YS
+    act(("pf0", 0, a1), ("W1", 0, a1), F.Copy, scale=S(45))
+    act(("pf1", 0, a1), ("W2", 0, a1), F.Copy, scale=S(46))
+    ts(("Y", 0, a1), ("B", 0, a1), S(44), A.mult)
+    tt(("Y", 0, a1), ("Y", 0, a1), ("pf0", 0, a1), A.add)
+    tt(("Y", 0, a1), ("Y", 0, a1), ("pf1", 0, a1), A.add)
+    dma("st1", T.y[:, 0:a1], T.Y[:, 0:a1], [("Y", 0, a1)], [])
+    act(("Y", a1, a2), ("B", a1, a2), F.Copy, scale=S(44))
+    act(("pf2", 0, a2 - a1), ("W1", a1, a2), F.Copy, scale=S(45))
+    act(("pf3", 0, a2 - a1), ("W2", a1, a2), F.Copy, scale=S(46))
+    tt(("Y", a1, a2), ("Y", a1, a2), ("pf2", 0, a2 - a1), A.add)
+    tt(("Y", a1, a2), ("Y", a1, a2), ("pf3", 0, a2 - a1), A.add)
+    dma("st2", T.y[:, a1:a2], T.Y[:, a1:a2], [("Y", a1, a2)], [])
+
+    for s in count:
+        g.wait_ge(T.sem[s], count[s])

@@ -4,7 +4,8 @@ from concourse.mybir import AluOpType, AxisListType, ActivationFunctionType
 
 W, HALO = 512, 10
 WX = W + HALO
-XS = [0, 192, 384, 448, WX]
+XS = [0, 150, 299, 448, WX]
+MODE = ["s", "s", "s", "2"]
 LD = 384
 YS = [0, 320, W]
 LEV = ["B", "H1", "W1", "XX", "W2", "H3"]
@@ -12,13 +13,13 @@ R18 = math.sqrt(18.0)
 ALPHA = [None, 2.0, 2.0, R18 + 2.0, R18 - 2.0, 2.0]
 SQ = 2.0 ** -8
 SLOT = 16
-DQ = {}
-TINY, EARLY = "s", 4
+TINY = "v"
+CY, GAP, REL2, RELH = 1.0e-3, 0.15, 0.5, 4.5
 
 SCRATCH = {"ACC": ("sbuf", [128, 48], "float32"), "R": ("sbuf", [128, 6 * SLOT], "float32"),
            "T1": ("sbuf", [128, 3 * SLOT], "float32"), "T2": ("sbuf", [128, SLOT], "float32"),
            "Z": ("sbuf", [128, SLOT], "float32"), "SM": ("sbuf", [128, 64], "float32"),
-           "JT": ("sbuf", [128, 48], "float32"),
+           "JT": ("sbuf", [128, 48], "float32"), "TN": ("sbuf", [128, WX], "float32"),
            "Y": ("sbuf", [128, W], "float32"), "PR": ("sbuf", [128, WX], "float32")}
 for _n in LEV + ["J0", "J1", "J2", "J3", "J4", "J5"]:
     SCRATCH[_n] = ("sbuf", [128, WX], "float32")
@@ -41,7 +42,7 @@ def rank_program(g, core, T, topo):
     left, right = cores[(rank - 1) % n], cores[(rank + 1) % n]
     A, F = AluOpType, ActivationFunctionType
     queues = {"v": g.vector, "s": g.scalar, "g": g, "y": g.sync}
-    hist, count = [], {}
+    hist, count, tasks = [], {}, []
     seen = {"v": {}, "s": {}, "g": {}, "y": {}}
 
     def ap(r):
@@ -52,18 +53,18 @@ def rank_program(g, core, T, topo):
             return False
         return (bank and a[0][0] == "p") or (a[1] < b[2] and b[1] < a[2])
 
-    def clash(q, reads, writes, h):
-        other = q != h[0]
+    def clash(q, reads, writes, hq, hr, hw):
+        other = q != hq
         for x in writes:
-            for o in h[3] + h[4]:
+            for o in hr + hw:
                 if over(x, o, other):
                     return True
         for x in reads:
-            for o in h[4]:
+            for o in hw:
                 if over(x, o, other):
                     return True
             if other and x[0][0] == "p":
-                for o in h[3]:
+                for o in hr:
                     if x[0] == o[0]:
                         return True
         return False
@@ -71,7 +72,7 @@ def rank_program(g, core, T, topo):
     def sync_to(q, reads, writes):
         need = {}
         for h in hist:
-            if seen[q].get(h[1], 0) < h[2] and need.get(h[1], 0) < h[2] and clash(q, reads, writes, h):
+            if seen[q].get(h[1], 0) < h[2] and need.get(h[1], 0) < h[2] and clash(q, reads, writes, h[0], h[3], h[4]):
                 need[h[1]] = h[2]
         for s in need:
             queues[q].wait_ge(T.sem[s], need[s])
@@ -81,11 +82,45 @@ def rank_program(g, core, T, topo):
         count[sem] = count.get(sem, 0) + inc
         hist.append((q, sem, count[sem], reads, writes))
 
-    def op(q, reads, writes, fn):
-        sync_to(q, reads, writes)
-        sem = "vdone" if q == "v" else "sdone"
-        fn().then_inc(T.sem[sem], 1)
-        note(q, sem, 1, reads, writes)
+    def op(q, reads, writes, fn, cost):
+        tasks.append((q, reads, writes, fn, max(cost, 64) * CY))
+
+    def flush():
+        m = len(tasks)
+        deps = [[j for j in range(i) if clash(tasks[i][0], tasks[i][1], tasks[i][2], tasks[j][0], tasks[j][1], tasks[j][2])]
+                for i in range(m)]
+        prio = [t[4] for t in tasks]
+        for i in range(m - 1, -1, -1):
+            for j in deps[i]:
+                prio[j] = max(prio[j], tasks[j][4] + GAP + prio[i])
+        rel = []
+        for t in tasks:
+            r = 0.0
+            for x in t[1]:
+                if x[0] == "B" and x[2] > LD:
+                    r = max(r, REL2)
+                if x[0] == "B" and x[2] > W:
+                    r = max(r, RELH)
+            rel.append(r)
+        end, free, left_ = {}, {"v": 0.0, "s": 0.0}, list(range(m))
+        while left_:
+            best = None
+            for i in left_:
+                if all(j in end for j in deps[i]):
+                    st = max([free[tasks[i][0]], rel[i]] + [end[j] + GAP for j in deps[i]])
+                    key = (st, -prio[i])
+                    if best is None or key < best[0]:
+                        best = (key, i)
+            i = best[1]
+            q, reads, writes, fn, cost = tasks[i]
+            end[i] = best[0][0] + cost
+            free[q] = end[i]
+            left_.remove(i)
+            sync_to(q, reads, writes)
+            sem = "vdone" if q == "v" else "sdone"
+            fn().then_inc(T.sem[sem], 1)
+            note(q, sem, 1, reads, writes)
+        del tasks[:]
 
     def val(x):
         return ap(x) if isinstance(x, tuple) else x
@@ -93,27 +128,32 @@ def rank_program(g, core, T, topo):
     def cols(*xs):
         return [x for x in xs if isinstance(x, tuple)]
 
+    def wid(r):
+        return r[2] - r[1]
+
     def act(out, in_, func, scale=1.0, bias=0.0, acc=None):
         def fn():
             if acc is not None:
                 return g.scalar.activation(ap(out), ap(in_), func, bias=val(bias), scale=val(scale), accum_out=ap(acc))
             return g.scalar.activation(ap(out), ap(in_), func, bias=val(bias), scale=val(scale))
-        op("s", [in_] + cols(scale, bias), [out] + cols(acc), fn)
+        op("s", [in_] + cols(scale, bias), [out] + cols(acc), fn, max(wid(in_), 64) + (24 if acc else 0))
 
     def tt(out, a, b, o):
-        op("v", [a, b], [out], lambda: g.vector.tensor_tensor(ap(out), ap(a), ap(b), o))
+        op("v", [a, b], [out], lambda: g.vector.tensor_tensor(ap(out), ap(a), ap(b), o),
+           wid(a) * (1 if "p" in (a[0][0], b[0][0]) else 2))
 
     def ts(out, a, s1, o1, s2=None, o2=None):
         if o2 is None:
-            op("v", [a] + cols(s1), [out], lambda: g.vector.tensor_scalar(ap(out), ap(a), val(s1), None, o1))
+            op("v", [a] + cols(s1), [out], lambda: g.vector.tensor_scalar(ap(out), ap(a), val(s1), None, o1), wid(a))
         else:
-            op("v", [a] + cols(s1, s2), [out], lambda: g.vector.tensor_scalar(ap(out), ap(a), val(s1), val(s2), o1, o2))
+            op("v", [a] + cols(s1, s2), [out],
+               lambda: g.vector.tensor_scalar(ap(out), ap(a), val(s1), val(s2), o1, o2), wid(a))
 
     def red(out, a, neg=False):
-        op("v", [a], [out], lambda: g.vector.tensor_reduce(ap(out), ap(a), AxisListType.X, A.add, negate=neg))
+        op("v", [a], [out], lambda: g.vector.tensor_reduce(ap(out), ap(a), AxisListType.X, A.add, negate=neg), wid(a))
 
     def cpy(out, a):
-        op("v", [a], [out], lambda: g.vector.tensor_copy(ap(out), ap(a)))
+        op("v", [a], [out], lambda: g.vector.tensor_copy(ap(out), ap(a)), wid(a))
 
     def dma(sem, out, in_, reads, writes):
         sync_to("y", reads, writes)
@@ -144,7 +184,6 @@ def rank_program(g, core, T, topo):
 
     dma("ld1", T.B[:, 0:LD], T.b[:, 0:LD], [], [("B", 0, LD)])
     dma("ld2", T.B[:, LD:W], T.b[:, LD:W], [], [("B", LD, W)])
-    op("v", [], [P(0, SLOT)], lambda: g.vector.memset(ap(P(0, SLOT)), 0.0))
     sync_to("g", [("B", 0, HALO)], [])
     rid, pid = topo.addr(left, core)
     m1 = topo.mask(core, left)
@@ -152,29 +191,30 @@ def rank_program(g, core, T, topo):
     count["sent"] = _bits(m1)
 
     NB = len(XS) - 1
-    last = NB - 1
 
     def rng(j, k):
         return (k if j == 0 else XS[j] - k), XS[j + 1] - k
 
-    def pd(j, lo, hi):
+    def bank(name, j, lo, hi):
         base = max(0, XS[j] - 8)
-        return ("pd%d" % j, lo - base, hi - base)
+        return (name % j, lo - base, hi - base)
 
-    def scale_(j, k):
+    def level(j, k):
         lo, hi = rng(j, k)
-        if DQ.get((j, k), "s" if j < 2 else "v") == "s":
-            act(pd(j, lo, hi), (LEV[k - 1], lo, hi), F.Copy, scale=ALPHA[k])
+        src, d, o = LEV[k - 1], bank("pd%d", j, lo, hi), (A.subtract if k == 4 else A.add)
+        if MODE[j] == "v":
+            ts(d, (src, lo, hi), ALPHA[k], A.mult)
         else:
-            ts(pd(j, lo, hi), (LEV[k - 1], lo, hi), ALPHA[k], A.mult)
-
-    def adds(j, k):
-        lo, hi = rng(j, k)
-        d, o = pd(j, lo, hi), (A.subtract if k == 4 else A.add)
+            act(d, (src, lo, hi), F.Copy, scale=ALPHA[k])
         if k == 5:
             tt(("PR", lo, hi), ("W1", lo, hi), d, A.mult)
-        tt(d, d, (LEV[k - 1], lo - 1, hi - 1), o)
-        tt((LEV[k], lo, hi), d, (LEV[k - 1], lo + 1, hi + 1), o)
+        if MODE[j] == "2":
+            tt(("TN", lo, hi), (src, lo - 1, hi - 1), (src, lo + 1, hi + 1), A.add)
+            tt((LEV[k], lo, hi), d, ("TN", lo, hi), o)
+        else:
+            x = bank("pf%d", j, lo, hi) if k == 5 else d
+            tt(x, d, (src, lo - 1, hi - 1), o)
+            tt((LEV[k], lo, hi), x, (src, lo + 1, hi + 1), o)
 
     def acc(m, j):
         return ("ACC", 8 * m + j, 8 * m + j + 1)
@@ -201,33 +241,26 @@ def rank_program(g, core, T, topo):
         else:
             act(out, a, F.Copy, scale=c)
 
-    extra = {1: 1, 2: 2, 3: 0, 4: 4}
-    scale_(0, 1); scale_(1, 1)
-    adds(0, 1); adds(1, 1)
-    for k in range(1, 5):
-        scale_(0, k + 1); sq(0, extra[k]); scale_(1, k + 1); sq(1, extra[k])
-        adds(0, k + 1); adds(1, k + 1)
-    sp(0); sq(0, 5); sp(1); sq(1, 5)
-    e = TINY
-    for j in range(2, NB):
+    op("v", [], [P(0, SLOT)], lambda: g.vector.memset(ap(P(0, SLOT)), 0.0), SLOT)
+    for j in range(NB):
         sq(j, 0)
-        for k in range(1, 6):
-            scale_(j, k); adds(j, k)
+    for k in range(1, 6):
+        for j in range(NB):
+            level(j, k)
             if k == 5:
                 sp(j)
             if k != 3:
                 sq(j, k)
-            if j == last and k == 2:
-                cpy(P(10, 2), ("W1", W, W + 2))
-            if j == last and k == EARLY:
-                total(e, P(5), 0); times(e, acc(1, NB), P(5), -18.0)
-                total(e, P(1), 1); times(e, acc(2, NB), P(1), -18.0)
-                total(e, P(8), 1, 1, True); total(e, P(4), 2, 1, True); times(e, acc(3, NB), P(4), -18.0)
-            if j == last and k == 4:
-                cpy(P(12, 4), ("W2", W, W + 4))
-    total("v", P(3), 4); times("v", acc(5, NB), P(3), -18.0)
-    total("v", P(0), 3); total("v", P(6), 3, 1, True)
+    e = TINY
+    cpy(P(10, 2), ("W1", W, W + 2))
+    cpy(P(12, 4), ("W2", W, W + 4))
+    total(e, P(5), 0); times(e, acc(1, NB), P(5), -18.0)
+    total(e, P(1), 1); times(e, acc(2, NB), P(1), -18.0)
+    total(e, P(8), 1, 1, True); total(e, P(4), 2, 1, True); times(e, acc(3, NB), P(4), -18.0)
+    total(e, P(3), 4); times(e, acc(5, NB), P(3), -18.0)
+    total(e, P(0), 3); total(e, P(6), 3, 1, True)
     total("v", P(2), 5, 1, True)
+    flush()
 
     sync_to("g", [P(0, SLOT)], [])
     mo, mi = masks(core)
@@ -272,7 +305,7 @@ def rank_program(g, core, T, topo):
     act(S(40), S(19), F.Copy, scale=-1.0)
     act(S(41), S(17), F.Copy, scale=S(40))
     act(S(35), S(16), F.Identity, scale=S(20), bias=S(41))
-    op("v", [S(32, 2)], [S(36, 2)], lambda: g.vector.reciprocal(ap(S(36, 2)), ap(S(32, 2))))
+    op("v", [S(32, 2)], [S(36, 2)], lambda: g.vector.reciprocal(ap(S(36, 2)), ap(S(32, 2))), 241)
     ts(S(45, 2), S(34, 2), S(37), A.mult, 4.0, A.mult)
     act(S(43), S(33), F.Copy, scale=S(42))
     act(S(48), S(34), F.Identity, scale=Z(4), bias=S(43))
@@ -286,12 +319,13 @@ def rank_program(g, core, T, topo):
     ts(("Y", 0, a1), ("B", 0, a1), S(44), A.mult)
     tt(("Y", 0, a1), ("Y", 0, a1), ("pf0", 0, a1), A.add)
     tt(("Y", 0, a1), ("Y", 0, a1), ("pf1", 0, a1), A.add)
-    dma("st1", T.y[:, 0:a1], T.Y[:, 0:a1], [("Y", 0, a1)], [])
     act(("Y", a1, a2), ("B", a1, a2), F.Copy, scale=S(44))
     act(("pf2", 0, a2 - a1), ("W1", a1, a2), F.Copy, scale=S(45))
     act(("pf3", 0, a2 - a1), ("W2", a1, a2), F.Copy, scale=S(46))
     tt(("Y", a1, a2), ("Y", a1, a2), ("pf2", 0, a2 - a1), A.add)
     tt(("Y", a1, a2), ("Y", a1, a2), ("pf3", 0, a2 - a1), A.add)
+    flush()
+    dma("st1", T.y[:, 0:a1], T.Y[:, 0:a1], [("Y", 0, a1)], [])
     dma("st2", T.y[:, a1:a2], T.Y[:, a1:a2], [("Y", a1, a2)], [])
 
     for s in count:

@@ -6,20 +6,20 @@ W, HALO = 512, 10
 WX = W + HALO
 XS = [0, 150, 299, 448, WX]
 MODE = ["s", "s", "s", "2"]
-LD = 384
-YS = [0, 320, W]
+LD = 320
+YS = [0, 352, W]
 LEV = ["B", "H1", "W1", "XX", "W2", "H3"]
 R18 = math.sqrt(18.0)
 ALPHA = [None, 2.0, 2.0, R18 + 2.0, R18 - 2.0, 2.0]
 SQ = 2.0 ** -8
 SLOT = 16
+GQ = (("v", 8), ("s", 4), ("v", 6), ("s", 5), ("v", 0), ("s", 3), ("v", 1), ("v", 2))
 TINY = "v"
-CY, GAP, REL2, RELH = 1.0e-3, 0.15, 0.5, 4.5
+CY, GAP, REL2, RELH = 1.0e-3, 0.22, 0.5, 4.5
 
 SCRATCH = {"ACC": ("sbuf", [128, 48], "float32"), "R": ("sbuf", [128, 6 * SLOT], "float32"),
-           "T1": ("sbuf", [128, 3 * SLOT], "float32"), "T2": ("sbuf", [128, SLOT], "float32"),
            "Z": ("sbuf", [128, SLOT], "float32"), "SM": ("sbuf", [128, 64], "float32"),
-           "JT": ("sbuf", [128, 48], "float32"), "TN": ("sbuf", [128, WX], "float32"),
+           "JT": ("sbuf", [128, 64], "float32"), "TL": ("sbuf", [128, WX], "float32"),
            "Y": ("sbuf", [128, W], "float32"), "PR": ("sbuf", [128, WX], "float32")}
 for _n in LEV + ["J0", "J1", "J2", "J3", "J4", "J5"]:
     SCRATCH[_n] = ("sbuf", [128, WX], "float32")
@@ -209,8 +209,8 @@ def rank_program(g, core, T, topo):
         if k == 5:
             tt(("PR", lo, hi), ("W1", lo, hi), d, A.mult)
         if MODE[j] == "2":
-            tt(("TN", lo, hi), (src, lo - 1, hi - 1), (src, lo + 1, hi + 1), A.add)
-            tt((LEV[k], lo, hi), d, ("TN", lo, hi), o)
+            tt(("TL", lo, hi), (src, lo - 1, hi - 1), (src, lo + 1, hi + 1), A.add)
+            tt((LEV[k], lo, hi), d, ("TL", lo, hi), o)
         else:
             x = bank("pf%d", j, lo, hi) if k == 5 else d
             tt(x, d, (src, lo - 1, hi - 1), o)
@@ -289,37 +289,48 @@ def rank_program(g, core, T, topo):
     lo_ = T.rank_of(left) * SLOT
     act(("W1", 0, 2), ("R", lo_ + 10, lo_ + 12), F.Copy)
     act(("W2", 0, 4), ("R", lo_ + 12, lo_ + 16), F.Copy)
-    tt(("T1", 0, 48), ("R", 0, 48), ("R", 48, 96), A.add)
-    tt(("T2", 0, 16), ("T1", 0, 16), ("T1", 16, 32), A.add)
-    tt(Z(0, 16), ("T2", 0, 16), ("T1", 32, 48), A.add)
-    act(S(8, 2), Z(4, 2), F.Copy, scale=Z(4))
+
+    def gather(q, c):
+        if q == "v":
+            op("v", [("R", 0, 6 * SLOT)], [Z(c)],
+               lambda: g.vector.tensor_reduce(ap(Z(c)), T.R[:, c:6 * SLOT:SLOT], AxisListType.X, A.add), 6)
+        else:
+            op("s", [("R", 0, 6 * SLOT)], [Z(c), ("JT", 6 * c, 6 * c + 6)],
+               lambda: g.scalar.activation(ap(("JT", 6 * c, 6 * c + 6)), T.R[:, c:6 * SLOT:SLOT], F.Copy,
+                                           accum_out=ap(Z(c))), 88)
+
+    for q, c in GQ:
+        gather(q, c)
     ts(S(0, 5), Z(0, 5), Z(8), A.mult)
+    act(S(8, 2), Z(4, 2), F.Copy, scale=Z(4))
     act(S(11, 2), Z(4, 2), F.Copy, scale=Z(6))
     ts(S(10), Z(6), Z(6), A.mult)
-    act(S(32), Z(8), F.Copy)
-    act(S(42), Z(5), F.Copy, scale=-1.0)
     tt(S(16, 5), S(0, 5), S(8, 5), A.subtract)
     act(S(26, 2), S(19, 2), F.Copy, scale=S(19))
     ts(S(24, 2), S(16, 2), S(18), A.mult)
+    ts(S(41), S(17), S(19), A.mult)
     tt(S(33, 2), S(24, 2), S(26, 2), A.subtract)
-    act(S(40), S(19), F.Copy, scale=-1.0)
-    act(S(41), S(17), F.Copy, scale=S(40))
-    act(S(35), S(16), F.Identity, scale=S(20), bias=S(41))
-    op("v", [S(32, 2)], [S(36, 2)], lambda: g.vector.reciprocal(ap(S(36, 2)), ap(S(32, 2))), 241)
-    ts(S(45, 2), S(34, 2), S(37), A.mult, 4.0, A.mult)
-    act(S(43), S(33), F.Copy, scale=S(42))
-    act(S(48), S(34), F.Identity, scale=Z(4), bias=S(43))
-    act(S(49), S(35), F.Identity, scale=Z(6), bias=S(48))
-    ts(S(50), S(36), S(37), A.mult, -4.0, A.mult)
-    ts(S(44), S(49), S(50), A.mult)
+    ts(S(35), S(16), S(20), A.mult, S(41), A.subtract)
+    ts(S(52, 2), Z(0, 2), Z(2), A.mult)
+    act(S(54, 2), Z(3, 2), F.Copy, scale=Z(3))
+    act(S(56), Z(0), F.Copy, scale=Z(4))
+    act(S(60), Z(5), F.Copy, scale=Z(8))
+    ts(S(61), Z(4), Z(8), A.mult, -1.0, A.mult)
+    act(S(62), Z(6), F.Copy, scale=Z(8))
+    tt(S(57, 2), S(52, 2), S(54, 2), A.subtract)
+    ts(S(59), Z(1), Z(3), A.mult, S(56), A.subtract)
+    tt(S(48, 3), S(57, 3), S(60, 3), A.mult)
+    red(S(36), S(48, 3))
+    op("v", [S(33)], [S(38)], lambda: g.vector.reciprocal(ap(S(38)), ap(S(33))), 235)
+    ts(S(45, 3), S(34, 3), S(38), A.mult, 4.0, A.mult)
 
     a0, a1, a2 = YS
     act(("pf0", 0, a1), ("W1", 0, a1), F.Copy, scale=S(45))
     act(("pf1", 0, a1), ("W2", 0, a1), F.Copy, scale=S(46))
-    ts(("Y", 0, a1), ("B", 0, a1), S(44), A.mult)
+    ts(("Y", 0, a1), ("B", 0, a1), S(47), A.mult)
     tt(("Y", 0, a1), ("Y", 0, a1), ("pf0", 0, a1), A.add)
     tt(("Y", 0, a1), ("Y", 0, a1), ("pf1", 0, a1), A.add)
-    act(("Y", a1, a2), ("B", a1, a2), F.Copy, scale=S(44))
+    act(("Y", a1, a2), ("B", a1, a2), F.Copy, scale=S(47))
     act(("pf2", 0, a2 - a1), ("W1", a1, a2), F.Copy, scale=S(45))
     act(("pf3", 0, a2 - a1), ("W2", a1, a2), F.Copy, scale=S(46))
     tt(("Y", a1, a2), ("Y", a1, a2), ("pf2", 0, a2 - a1), A.add)

import math
from concourse.bass import DstId, RemoteDMATransfer
from concourse.mybir import AluOpType, AxisListType, ActivationFunctionType

W, HALO = 512, 10
WX = W + HALO
XS = [0, 150, 299, 448, WX]
MODE = ["s", "s", "s", "2"]
LD = 320
YS = [0, 352, W]
LEV = ["B", "H1", "W1", "XX", "W2", "H3"]
R18 = math.sqrt(18.0)
ALPHA = [None, 2.0, 2.0, R18 + 2.0, R18 - 2.0, 2.0]
SQ = 2.0 ** -8
SLOT = 16
GQ = (("v", 8), ("s", 4), ("v", 6), ("s", 5), ("v", 0), ("s", 3), ("v", 1), ("v", 2))
TINY = "v"
CY, GAP, REL2, RELH = 1.0e-3, 0.22, 0.5, 4.5

SCRATCH = {"ACC": ("sbuf", [128, 48], "float32"), "R": ("sbuf", [128, 6 * SLOT], "float32"),
           "Z": ("sbuf", [128, SLOT], "float32"), "SM": ("sbuf", [128, 64], "float32"),
           "JT": ("sbuf", [128, 64], "float32"), "TL": ("sbuf", [128, WX], "float32"),
           "Y": ("sbuf", [128, W], "float32"), "PR": ("sbuf", [128, WX], "float32")}
for _n in LEV + ["J0", "J1", "J2", "J3", "J4", "J5"]:
    SCRATCH[_n] = ("sbuf", [128, WX], "float32")
for _j in range(4):
    SCRATCH["pd%d" % _j] = ("psum", [128, 512], "float32")
    SCRATCH["pf%d" % _j] = ("psum", [128, 512], "float32")
SEMAPHORES = ["ld1", "ld2", "halo", "arr", "sent", "st1", "st2", "vdone", "sdone"]


def _bits(m):
    return sum((m >> i) & 1 for i in range(32))


def rank_program(g, core, T, topo):
    rank = T.rank_of(core)
    if rank is None:
        return
    cores = list(T.cores)
    n = len(cores)
    left, right = cores[(rank - 1) % n], cores[(rank + 1) % n]
    A, F = AluOpType, ActivationFunctionType
    queues = {"v": g.vector, "s": g.scalar, "g": g, "y": g.sync}
    hist, count, tasks = [], {}, []
    seen = {"v": {}, "s": {}, "g": {}, "y": {}}

    def ap(r):
        return T[r[0]][:, r[1]:r[2]]

    def over(a, b, bank):
        if a[0] != b[0]:
            return False
        return (bank and a[0][0] == "p") or (a[1] < b[2] and b[1] < a[2])

    def clash(q, reads, writes, hq, hr, hw):
        other = q != hq
        for x in writes:
            for o in hr + hw:
                if over(x, o, other):
                    return True
        for x in reads:
            for o in hw:
                if over(x, o, other):
                    return True
            if other and x[0][0] == "p":
                for o in hr:
                    if x[0] == o[0]:
                        return True
        return False

    def sync_to(q, reads, writes):
        need = {}
        for h in hist:
            if seen[q].get(h[1], 0) < h[2] and need.get(h[1], 0) < h[2] and clash(q, reads, writes, h[0], h[3], h[4]):
                need[h[1]] = h[2]
        for s in need:
            queues[q].wait_ge(T.sem[s], need[s])
            seen[q][s] = need[s]

    def note(q, sem, inc, reads, writes):
        count[sem] = count.get(sem, 0) + inc
        hist.append((q, sem, count[sem], reads, writes))

    def op(q, reads, writes, fn, cost):
        tasks.append((q, reads, writes, fn, max(cost, 64) * CY))

    def flush():
        m = len(tasks)
        deps = [[j for j in range(i) if clash(tasks[i][0], tasks[i][1], tasks[i][2], tasks[j][0], tasks[j][1], tasks[j][2])]
                for i in range(m)]
        prio = [t[4] for t in tasks]
        for i in range(m - 1, -1, -1):
            for j in deps[i]:
                prio[j] = max(prio[j], tasks[j][4] + GAP + prio[i])
        rel = []
        for t in tasks:
            r = 0.0
            for x in t[1]:
                if x[0] == "B" and x[2] > LD:
                    r = max(r, REL2)
                if x[0] == "B" and x[2] > W:
                    r = max(r, RELH)
            rel.append(r)
        end, free, left_ = {}, {"v": 0.0, "s": 0.0}, list(range(m))
        while left_:
            best = None
            for i in left_:
                if all(j in end for j in deps[i]):
                    st = max([free[tasks[i][0]], rel[i]] + [end[j] + GAP for j in deps[i]])
                    key = (st, -prio[i])
                    if best is None or key < best[0]:
                        best = (key, i)
            i = best[1]
            q, reads, writes, fn, cost = tasks[i]
            end[i] = best[0][0] + cost
            free[q] = end[i]
            left_.remove(i)
            sync_to(q, reads, writes)
            sem = "vdone" if q == "v" else "sdone"
            fn().then_inc(T.sem[sem], 1)
            note(q, sem, 1, reads, writes)
        del tasks[:]

    def val(x):
        return ap(x) if isinstance(x, tuple) else x

    def cols(*xs):
        return [x for x in xs if isinstance(x, tuple)]

    def wid(r):
        return r[2] - r[1]

    def act(out, in_, func, scale=1.0, bias=0.0, acc=None):
        def fn():
            if acc is not None:
                return g.scalar.activation(ap(out), ap(in_), func, bias=val(bias), scale=val(scale), accum_out=ap(acc))
            return g.scalar.activation(ap(out), ap(in_), func, bias=val(bias), scale=val(scale))
        op("s", [in_] + cols(scale, bias), [out] + cols(acc), fn, max(wid(in_), 64) + (24 if acc else 0))

    def tt(out, a, b, o):
        op("v", [a, b], [out], lambda: g.vector.tensor_tensor(ap(out), ap(a), ap(b), o),
           wid(a) * (1 if "p" in (a[0][0], b[0][0]) else 2))

    def ts(out, a, s1, o1, s2=None, o2=None):
        if o2 is None:
            op("v", [a] + cols(s1), [out], lambda: g.vector.tensor_scalar(ap(out), ap(a), val(s1), None, o1), wid(a))
        else:
            op("v", [a] + cols(s1, s2), [out],
               lambda: g.vector.tensor_scalar(ap(out), ap(a), val(s1), val(s2), o1, o2), wid(a))

    def red(out, a, neg=False):
        op("v", [a], [out], lambda: g.vector.tensor_reduce(ap(out), ap(a), AxisListType.X, A.add, negate=neg), wid(a))

    def cpy(out, a):
        op("v", [a], [out], lambda: g.vector.tensor_copy(ap(out), ap(a)), wid(a))

    def dma(sem, out, in_, reads, writes):
        sync_to("y", reads, writes)
        g.sync.dma_start(out, in_).then_inc(T.sem[sem], 16)
        note("y", sem, 16, reads, writes)

    own = rank * SLOT

    def P(c, w=1):
        return ("R", own + c, own + c + w)

    others = [c for c in cores if c != core]
    off = [c for c in others if (topo.host(c), topo.chip(c)) != (topo.host(core), topo.chip(core))]
    on = [c for c in others if c not in off]

    def masks(src):
        o = [c for c in cores if c != src and (topo.host(c), topo.chip(c)) != (topo.host(src), topo.chip(src))]
        i = [c for c in cores if c != src and c not in o]
        mo = topo.mask(src, o[0])
        return mo, topo.mask(src, i[0]) & ~mo

    note("x", "halo", _bits(topo.mask(right, core)), [], [("B", W, WX)])
    arrive = 0
    for c in others:
        mo, mi = masks(c)
        arrive += _bits(mo if c in off else mi)
    note("x", "arr", arrive, [], [("R", T.rank_of(c) * SLOT, T.rank_of(c) * SLOT + SLOT) for c in others])

    dma("ld1", T.B[:, 0:LD], T.b[:, 0:LD], [], [("B", 0, LD)])
    dma("ld2", T.B[:, LD:W], T.b[:, LD:W], [], [("B", LD, W)])
    sync_to("g", [("B", 0, HALO)], [])
    rid, pid = topo.addr(left, core)
    m1 = topo.mask(core, left)
    g.remote_dma(T.B[:, W:WX], T.B[:, 0:HALO], T.sem.halo, T.sem.sent, pid, rid, m1)
    count["sent"] = _bits(m1)

    NB = len(XS) - 1

    def rng(j, k):
        return (k if j == 0 else XS[j] - k), XS[j + 1] - k

    def bank(name, j, lo, hi):
        base = max(0, XS[j] - 8)
        return (name % j, lo - base, hi - base)

    def level(j, k):
        lo, hi = rng(j, k)
        src, d, o = LEV[k - 1], bank("pd%d", j, lo, hi), (A.subtract if k == 4 else A.add)
        if MODE[j] == "v":
            ts(d, (src, lo, hi), ALPHA[k], A.mult)
        else:
            act(d, (src, lo, hi), F.Copy, scale=ALPHA[k])
        if k == 5:
            tt(("PR", lo, hi), ("W1", lo, hi), d, A.mult)
        if MODE[j] == "2":
            tt(("TL", lo, hi), (src, lo - 1, hi - 1), (src, lo + 1, hi + 1), A.add)
            tt((LEV[k], lo, hi), d, ("TL", lo, hi), o)
        else:
            x = bank("pf%d", j, lo, hi) if k == 5 else d
            tt(x, d, (src, lo - 1, hi - 1), o)
            tt((LEV[k], lo, hi), x, (src, lo + 1, hi + 1), o)

    def acc(m, j):
        return ("ACC", 8 * m + j, 8 * m + j + 1)

    def sq(j, k):
        lo, hi = rng(j, k) if k else (XS[j], XS[j + 1])
        hi = min(hi, W + k)
        act(("J%d" % k, lo, hi), (LEV[k], lo, hi), F.Square, scale=SQ, acc=acc(k, j))

    def sp(j):
        lo, hi = rng(j, 5)
        act(("J3", lo, hi), ("PR", lo, hi), F.Copy, scale=0.5 * SQ * SQ, acc=acc(3, j))

    def total(q, out, m, more=0, neg=False):
        src = ("ACC", 8 * m, 8 * m + NB + more)
        if q == "v":
            red(out, src, neg)
        else:
            act(("JT", 8 * m, 8 * m + NB + more), src, F.Copy, scale=(-1.0 if neg else 1.0), acc=out)

    def times(q, out, a, c):
        if q == "v":
            ts(out, a, c, A.mult)
        else:
            act(out, a, F.Copy, scale=c)

    op("v", [], [P(0, SLOT)], lambda: g.vector.memset(ap(P(0, SLOT)), 0.0), SLOT)
    for j in range(NB):
        sq(j, 0)
    for k in range(1, 6):
        for j in range(NB):
            level(j, k)
            if k == 5:
                sp(j)
            if k != 3:
                sq(j, k)
    e = TINY
    cpy(P(10, 2), ("W1", W, W + 2))
    cpy(P(12, 4), ("W2", W, W + 4))
    total(e, P(5), 0); times(e, acc(1, NB), P(5), -18.0)
    total(e, P(1), 1); times(e, acc(2, NB), P(1), -18.0)
    total(e, P(8), 1, 1, True); total(e, P(4), 2, 1, True); times(e, acc(3, NB), P(4), -18.0)
    total(e, P(3), 4); times(e, acc(5, NB), P(3), -18.0)
    total(e, P(0), 3); total(e, P(6), 3, 1, True)
    total("v", P(2), 5, 1, True)
    flush()

    sync_to("g", [P(0, SLOT)], [])
    mo, mi = masks(core)

    def transfer(dsts, m):
        ids = []
        for c in dsts:
            r_, p_ = topo.addr(c, core)
            ids.append(DstId(rid=r_, pnc=p_))
        return RemoteDMATransfer(dst_ids=ids, dma_engine_mask=m, remote_sem=T.sem.arr, srcs=[ap(P(0, SLOT))],
                                 dsts=[ap(P(0, SLOT)) for c in dsts], alu_op=0)

    if mi & ~m1:
        g.remote_dma_fused([transfer(off, mo)], local_sem=T.sem.sent)
        g.remote_dma_fused([transfer(on, mi)], local_sem=T.sem.sent)
    else:
        g.remote_dma_fused([transfer(off, mo), transfer(on, mi)], local_sem=T.sem.sent)
    count["sent"] += _bits(mo) + _bits(mi)

    def S(c, w=1):
        return ("SM", c, c + w)

    def Z(c, w=1):
        return ("Z", c, c + w)

    lo_ = T.rank_of(left) * SLOT
    act(("W1", 0, 2), ("R", lo_ + 10, lo_ + 12), F.Copy)
    act(("W2", 0, 4), ("R", lo_ + 12, lo_ + 16), F.Copy)

    def gather(q, c):
        if q == "v":
            op("v", [("R", 0, 6 * SLOT)], [Z(c)],
               lambda: g.vector.tensor_reduce(ap(Z(c)), T.R[:, c:6 * SLOT:SLOT], AxisListType.X, A.add), 6)
        else:
            op("s", [("R", 0, 6 * SLOT)], [Z(c), ("JT", 6 * c, 6 * c + 6)],
               lambda: g.scalar.activation(ap(("JT", 6 * c, 6 * c + 6)), T.R[:, c:6 * SLOT:SLOT], F.Copy,
                                           accum_out=ap(Z(c))), 88)

    for q, c in GQ:
        gather(q, c)
    ts(S(0, 5), Z(0, 5), Z(8), A.mult)
    act(S(8, 2), Z(4, 2), F.Copy, scale=Z(4))
    act(S(11, 2), Z(4, 2), F.Copy, scale=Z(6))
    ts(S(10), Z(6), Z(6), A.mult)
    tt(S(16, 5), S(0, 5), S(8, 5), A.subtract)
    act(S(26, 2), S(19, 2), F.Copy, scale=S(19))
    ts(S(24, 2), S(16, 2), S(18), A.mult)
    ts(S(41), S(17), S(19), A.mult)
    tt(S(33, 2), S(24, 2), S(26, 2), A.subtract)
    ts(S(35), S(16), S(20), A.mult, S(41), A.subtract)
    ts(S(52, 2), Z(0, 2), Z(2), A.mult)
    act(S(54, 2), Z(3, 2), F.Copy, scale=Z(3))
    act(S(56), Z(0), F.Copy, scale=Z(4))
    act(S(60), Z(5), F.Copy, scale=Z(8))
    ts(S(61), Z(4), Z(8), A.mult, -1.0, A.mult)
    act(S(62), Z(6), F.Copy, scale=Z(8))
    tt(S(57, 2), S(52, 2), S(54, 2), A.subtract)
    ts(S(59), Z(1), Z(3), A.mult, S(56), A.subtract)
    tt(S(48, 3), S(57, 3), S(60, 3), A.mult)
    red(S(36), S(48, 3))
    op("v", [S(33)], [S(38)], lambda: g.vector.reciprocal(ap(S(38)), ap(S(33))), 235)
    ts(S(45, 3), S(34, 3), S(38), A.mult, 4.0, A.mult)

    a0, a1, a2 = YS
    act(("pf0", 0, a1), ("W1", 0, a1), F.Copy, scale=S(45))
    act(("pf1", 0, a1), ("W2", 0, a1), F.Copy, scale=S(46))
    ts(("Y", 0, a1), ("B", 0, a1), S(47), A.mult)
    tt(("Y", 0, a1), ("Y", 0, a1), ("pf0", 0, a1), A.add)
    tt(("Y", 0, a1), ("Y", 0, a1), ("pf1", 0, a1), A.add)
    act(("Y", a1, a2), ("B", a1, a2), F.Copy, scale=S(47))
    act(("pf2", 0, a2 - a1), ("W1", a1, a2), F.Copy, scale=S(45))
    act(("pf3", 0, a2 - a1), ("W2", a1, a2), F.Copy, scale=S(46))
    tt(("Y", a1, a2), ("Y", a1, a2), ("pf2", 0, a2 - a1), A.add)
    tt(("Y", a1, a2), ("Y", a1, a2), ("pf3", 0, a2 - a1), A.add)
    flush()
    dma("st1", T.y[:, 0:a1], T.Y[:, 0:a1], [("Y", 0, a1)], [])
    dma("st2", T.y[:, a1:a2], T.Y[:, a1:a2], [("Y", a1, a2)], [])

    for s in count:
        g.wait_ge(T.sem[s], count[s])
